import numpy as np
import ml_dtypes


def mxq(x, axis, fmt="e4m3"):
    dtype, down = {"e4m3": (ml_dtypes.float8_e4m3fn, 7), "e5m2": (ml_dtypes.float8_e5m2, 14)}[fmt]
    v = np.moveaxis(np.asarray(x, np.float32).astype(ml_dtypes.bfloat16).astype(np.float64), axis, -1)
    blocks = v.reshape(v.shape[:-1] + (-1, 32))
    amax = np.abs(blocks).max(-1, keepdims=True)
    byte = np.maximum(np.where(amax > 0, np.frexp(amax)[1] - 1 + 127, 0) - down, 1)
    scale = np.exp2(byte - 127.0)
    codes = (blocks / scale).astype(np.float32).astype(dtype).astype(np.float64)
    return np.moveaxis((codes * scale).reshape(v.shape), -1, axis)


WIDE = False


def mx_kscale(k):
    if not WIDE:
        return np.ones(k)
    levels = np.array([10, -10, 5, -5, 0])
    if k % 512:
        return np.exp2(np.random.permutation(np.resize(levels, k // 32))).repeat(32)
    a = np.empty((k // 512, 16))
    for p in range(k // 512):
        a[p, :8] = np.random.permutation(np.resize(levels, 8))
        for g in range(8):
            far = levels[np.abs(levels - a[p, g]) >= 10]
            a[p, g + 8] = far[np.random.randint(len(far))]
    return np.exp2(a.ravel()).repeat(32)


def f64(x):
    return np.asarray(x).astype(np.float64)


def striped(idx):
    return np.tile(idx.reshape(-1, 16).T, (8, 1)).astype(np.uint16)


def unstriped(offs):
    return offs[:16].T.reshape(-1).astype(np.int64)


K, T, E, C, N = 2048, 1024, 4, 128, 128


def by_expert(wq, xq):
    return np.concatenate([wq[e].T @ xq[:, e * C:(e + 1) * C] for e in range(E)], axis=1)


def setup_inputs():
    n = np.random.standard_normal
    s = mx_kscale(K)[:, None]
    return {
        "xT": (n((K, T)) * s).astype(np.float32),
        "w": (n((E, K, N)) / np.sqrt(K) / s[None]).astype(np.float32),
        "gate": np.tile(np.random.uniform(0.2, 1.0, E * C), (N, 1)).astype(np.float32),
        "offs": striped(np.random.permutation(T)[:E * C]),
    }


def reference(xT, w, gate, offs):
    idx = unstriped(offs)
    xq = mxq(f64(xT)[:, idx], 0, "e4m3")
    y = by_expert(mxq(f64(w), 1, "e4m3"), xq)
    out = np.zeros((N, T))
    out[:, idx] = f64(gate) * y
    return out

@@ -1,0 +1,135 @@
+from contextlib import ExitStack
+
+import concourse.mybir as mybir
+
+K, T, E, C, N = 2048, 1024, 4, 128, 128
+SLOTS = E * C
+FLOPS = 2 * K * N * SLOTS
+
+F32 = mybir.dt.float32
+BF16 = mybir.dt.bfloat16
+U32 = mybir.dt.uint32
+U16 = mybir.dt.uint16
+U8 = mybir.dt.uint8
+FP8X4 = mybir.dt.float8_e4m3fn_x4
+MULT = mybir.AluOpType.mult
+
+P = 128
+PACK = 4
+K_PASS = P * PACK
+PASSES = K // K_PASS
+HALF = 256
+HALVES = SLOTS // HALF
+
+
+def tile_routed_moe_kernel(tc, xT, w, gate, offs, out):
+    nc = tc.nc
+    with ExitStack() as ctx:
+        held = ctx.enter_context(tc.tile_pool(name="held", bufs=1))
+        ring = ctx.enter_context(tc.tile_pool(name="ring", bufs=4))
+        psum = ctx.enter_context(tc.psum_pool(name="psum", bufs=1))
+
+        offsets = held.tile([P, SLOTS // 16], U16, name="offsets")
+        nc.sync.dma_start(offsets[:], offs)
+
+        window = held.tile([N, T], F32, name="window")
+        nc.vector.memset(window[:], 0.0)
+
+        x_view = xT.rearrange("(g p t) n -> g p t n", p=P, t=PACK)
+        w_view = w.rearrange("e (g p t) n -> e p g (t n)", p=P, t=PACK)
+
+        planes = []
+        for g in range(PASSES):
+            row = []
+            for t in range(PACK):
+                plane = held.tile([P, T], F32, name="plane%d_%d" % (g, t))
+                row.append(plane)
+            planes.append(row)
+        w_raw = []
+        for e in range(E):
+            raw = held.tile([P, PASSES, PACK * N], F32, name="w_raw%d" % e)
+            w_raw.append(raw)
+        gate_sb = held.tile([N, SLOTS], F32, name="gate_sb")
+
+        def load_pass(g):
+            for t in range(PACK):
+                nc.sync.dma_start(out=planes[g][t][:], in_=x_view[g, :, t, :])
+
+        load_pass(0)
+        load_pass(1)
+        nc.sync.dma_start(out=w_raw[0][:], in_=w_view[0])
+        load_pass(2)
+        load_pass(3)
+        nc.sync.dma_start(out=gate_sb[:], in_=gate)
+        nc.sync.dma_start(out=w_raw[1][:], in_=w_view[1])
+        nc.sync.dma_start(out=w_raw[2][:], in_=w_view[2])
+        for g in range(PASSES):
+            nc.sync.dma_start(out=w_raw[3][:, g, :], in_=w_view[3, :, g, :])
+
+        x_codes = held.tile([P, PASSES, SLOTS], U32, name="x_codes", align_bytes=64)
+        x_scales = held.tile([P, PASSES, SLOTS], U8, name="x_scales", align_bytes=64)
+        w_codes = held.tile([P, E, PASSES * N], U32, name="w_codes", align_bytes=64)
+        w_scales = held.tile([P, E, PASSES * N], U8, name="w_scales", align_bytes=64)
+        sums = held.tile([N, SLOTS], F32, name="sums")
+
+        for g in range(PASSES):
+            halves = []
+            for h in range(HALVES):
+                gathered = ring.tile([P, PACK, HALF], F32, name="gathered")
+                halves.append(gathered)
+            for t in range(PACK):
+                for h in range(HALVES):
+                    nc.vector.tensor_copy(
+                        halves[h][:, t, :],
+                        planes[g][t][:].indirect(offsets[:, h * (HALF // 16) : (h + 1) * (HALF // 16)]),
+                    )
+            for h in range(HALVES):
+                cols = slice(h * HALF, (h + 1) * HALF)
+                grouped = ring.tile([P, HALF, PACK], BF16, name="grouped", align_bytes=64)
+                nc.scalar.copy(out=grouped[:], in_=halves[h][:].rearrange("p t n -> p n t"))
+                nc.vector.quantize_mx(
+                    out=x_codes[:, g, cols].bitcast(FP8X4),
+                    scales=x_scales[:, g, cols],
+                    in_=grouped[:].rearrange("p n t -> p (n t)"),
+                )
+
+        for e in range(E):
+            w_grouped = held.tile([P, PASSES, N, PACK], BF16, name="w_grouped%d" % e, align_bytes=64)
+            for g in range(PASSES):
+                nc.scalar.copy(
+                    out=w_grouped[:, g, :, :],
+                    in_=w_raw[e][:, g, :].rearrange("p (t n) -> p n t", t=PACK),
+                )
+                if e == E - 1:
+                    nc.vector.quantize_mx(
+                        out=w_codes[:, e, g * N : (g + 1) * N].bitcast(FP8X4),
+                        scales=w_scales[:, e, g * N : (g + 1) * N],
+                        in_=w_grouped[:, g, :, :].rearrange("p n t -> p (n t)"),
+                    )
+            if e < E - 1:
+                nc.vector.quantize_mx(
+                    out=w_codes[:, e, :].bitcast(FP8X4),
+                    scales=w_scales[:, e, :],
+                    in_=w_grouped[:].rearrange("p g n t -> p (g n t)"),
+                )
+            acc = psum.tile([N, C], F32, name="acc%d" % e)
+            cols = slice(e * C, (e + 1) * C)
+            for g in range(PASSES):
+                nc.tensor.matmul_mx(
+                    out=acc[:],
+                    lhsT=w_codes[:, e, g * N : (g + 1) * N].bitcast(FP8X4),
+                    lhsT_scale=w_scales[:, e, g * N : (g + 1) * N],
+                    rhs=x_codes[:, g, cols].bitcast(FP8X4),
+                    rhs_scale=x_scales[:, g, cols],
+                    start=(g == 0),
+                    stop=(g == PASSES - 1),
+                )
+            nc.scalar.copy(out=sums[:, cols], in_=acc[:])
+            nc.vector.tensor_tensor(
+                window[:].indirect(offsets[:, e * (C // 16) : (e + 1) * (C // 16)]),
+                sums[:, cols],
+                gate_sb[:, cols],
+                MULT,
+            )
+
+        nc.sync.dma_start(out=out, in_=window[:])

@@ -18,15 +18,12 @@ P = 128
 PACK = 4
 K_PASS = P * PACK
 PASSES = K // K_PASS
-HALF = 256
-HALVES = SLOTS // HALF
 
 
 def tile_routed_moe_kernel(tc, xT, w, gate, offs, out):
     nc = tc.nc
     with ExitStack() as ctx:
         held = ctx.enter_context(tc.tile_pool(name="held", bufs=1))
-        ring = ctx.enter_context(tc.tile_pool(name="ring", bufs=4))
         psum = ctx.enter_context(tc.psum_pool(name="psum", bufs=1))
 
         offsets = held.tile([P, SLOTS // 16], U16, name="offsets")
@@ -38,80 +35,73 @@ def tile_routed_moe_kernel(tc, xT, w, gate, offs, out):
         x_view = xT.rearrange("(g p t) n -> g p t n", p=P, t=PACK)
         w_view = w.rearrange("e (g p t) n -> e p g (t n)", p=P, t=PACK)
 
-        planes = []
+        x_raw = []
+        x_grouped = []
         for g in range(PASSES):
-            row = []
-            for t in range(PACK):
-                plane = held.tile([P, T], F32, name="plane%d_%d" % (g, t))
-                row.append(plane)
-            planes.append(row)
+            raw = held.tile([P, PACK, T], F32, name="x_raw%d" % g)
+            x_raw.append(raw)
+            grouped = held.tile([P, SLOTS, PACK], BF16, name="x_grouped%d" % g, align_bytes=64)
+            x_grouped.append(grouped)
         w_raw = []
+        w_grouped = []
         for e in range(E):
             raw = held.tile([P, PASSES, PACK * N], F32, name="w_raw%d" % e)
             w_raw.append(raw)
+            grouped = held.tile([P, PASSES, N, PACK], BF16, name="w_grouped%d" % e, align_bytes=64)
+            w_grouped.append(grouped)
         gate_sb = held.tile([N, SLOTS], F32, name="gate_sb")
-
-        def load_pass(g):
-            for t in range(PACK):
-                nc.sync.dma_start(out=planes[g][t][:], in_=x_view[g, :, t, :])
-
-        load_pass(0)
-        load_pass(1)
-        nc.sync.dma_start(out=w_raw[0][:], in_=w_view[0])
-        load_pass(2)
-        load_pass(3)
-        nc.sync.dma_start(out=gate_sb[:], in_=gate)
-        nc.sync.dma_start(out=w_raw[1][:], in_=w_view[1])
-        nc.sync.dma_start(out=w_raw[2][:], in_=w_view[2])
-        for g in range(PASSES):
-            nc.sync.dma_start(out=w_raw[3][:, g, :], in_=w_view[3, :, g, :])
-
         x_codes = held.tile([P, PASSES, SLOTS], U32, name="x_codes", align_bytes=64)
         x_scales = held.tile([P, PASSES, SLOTS], U8, name="x_scales", align_bytes=64)
         w_codes = held.tile([P, E, PASSES * N], U32, name="w_codes", align_bytes=64)
         w_scales = held.tile([P, E, PASSES * N], U8, name="w_scales", align_bytes=64)
         sums = held.tile([N, SLOTS], F32, name="sums")
 
-        for g in range(PASSES):
-            halves = []
-            for h in range(HALVES):
-                gathered = ring.tile([P, PACK, HALF], F32, name="gathered")
-                halves.append(gathered)
+        def load_x(g):
             for t in range(PACK):
-                for h in range(HALVES):
-                    nc.vector.tensor_copy(
-                        halves[h][:, t, :],
-                        planes[g][t][:].indirect(offsets[:, h * (HALF // 16) : (h + 1) * (HALF // 16)]),
-                    )
-            for h in range(HALVES):
-                cols = slice(h * HALF, (h + 1) * HALF)
-                grouped = ring.tile([P, HALF, PACK], BF16, name="grouped", align_bytes=64)
-                nc.scalar.copy(out=grouped[:], in_=halves[h][:].rearrange("p t n -> p n t"))
-                nc.vector.quantize_mx(
-                    out=x_codes[:, g, cols].bitcast(FP8X4),
-                    scales=x_scales[:, g, cols],
-                    in_=grouped[:].rearrange("p n t -> p (n t)"),
-                )
+                nc.sync.dma_start(out=x_raw[g][:, t, :], in_=x_view[g, :, t, :])
 
-        for e in range(E):
-            w_grouped = held.tile([P, PASSES, N, PACK], BF16, name="w_grouped%d" % e, align_bytes=64)
-            for g in range(PASSES):
-                nc.scalar.copy(
-                    out=w_grouped[:, g, :, :],
-                    in_=w_raw[e][:, g, :].rearrange("p (t n) -> p n t", t=PACK),
-                )
-                if e == E - 1:
-                    nc.vector.quantize_mx(
-                        out=w_codes[:, e, g * N : (g + 1) * N].bitcast(FP8X4),
-                        scales=w_scales[:, e, g * N : (g + 1) * N],
-                        in_=w_grouped[:, g, :, :].rearrange("p n t -> p (n t)"),
-                    )
-            if e < E - 1:
-                nc.vector.quantize_mx(
-                    out=w_codes[:, e, :].bitcast(FP8X4),
-                    scales=w_scales[:, e, :],
-                    in_=w_grouped[:].rearrange("p g n t -> p (g n t)"),
-                )
+        def load_w(e, g0, g1):
+            nc.sync.dma_start(out=w_raw[e][:, g0:g1, :], in_=w_view[e, :, g0:g1, :])
+
+        load_x(0)
+        load_w(0, 0, 2)
+        load_x(1)
+        load_w(0, 2, 4)
+        load_x(2)
+        load_w(1, 0, 2)
+        load_x(3)
+        load_w(1, 2, 4)
+        nc.sync.dma_start(out=gate_sb[:], in_=gate)
+        load_w(2, 0, 2)
+        load_w(2, 2, 4)
+        load_w(3, 0, 2)
+        load_w(3, 2, 3)
+        load_w(3, 3, 4)
+
+        def gather(g, t):
+            nc.vector.tensor_copy(x_grouped[g][:, :, t], x_raw[g][:, t, :].indirect(offsets[:]))
+
+        def quantize_x(g):
+            nc.vector.quantize_mx(
+                out=x_codes[:, g, :].bitcast(FP8X4),
+                scales=x_scales[:, g, :],
+                in_=x_grouped[g][:].rearrange("p n t -> p (n t)"),
+            )
+
+        def group_w(e, g):
+            nc.scalar.copy(
+                out=w_grouped[e][:, g, :, :].rearrange("p (c i) t -> p c t i", i=4),
+                in_=w_raw[e][:, g, :].rearrange("p (t c i) -> p c t i", t=PACK, i=4),
+            )
+
+        def quantize_w(e, g0, g1):
+            nc.vector.quantize_mx(
+                out=w_codes[:, e, g0 * N : g1 * N].bitcast(FP8X4),
+                scales=w_scales[:, e, g0 * N : g1 * N],
+                in_=w_grouped[e][:, g0:g1, :, :].rearrange("p g n t -> p (g n t)"),
+            )
+
+        def multiply(e):
             acc = psum.tile([N, C], F32, name="acc%d" % e)
             cols = slice(e * C, (e + 1) * C)
             for g in range(PASSES):
@@ -125,11 +115,58 @@ def tile_routed_moe_kernel(tc, xT, w, gate, offs, out):
                     stop=(g == PASSES - 1),
                 )
             nc.scalar.copy(out=sums[:, cols], in_=acc[:])
+
+        def scatter(e):
+            cols = slice(e * C, (e + 1) * C)
             nc.vector.tensor_tensor(
                 window[:].indirect(offsets[:, e * (C // 16) : (e + 1) * (C // 16)]),
                 sums[:, cols],
                 gate_sb[:, cols],
                 MULT,
             )
+
+        for t in range(PACK):
+            gather(0, t)
+        group_w(0, 0)
+        group_w(0, 1)
+        gather(1, 0)
+        quantize_x(0)
+        for t in range(1, PACK):
+            gather(1, t)
+        group_w(0, 2)
+        group_w(0, 3)
+        gather(2, 0)
+        quantize_x(1)
+        quantize_w(0, 0, 4)
+        for t in range(1, PACK):
+            gather(2, t)
+        group_w(1, 0)
+        group_w(1, 1)
+        gather(3, 0)
+        quantize_x(2)
+        for t in range(1, PACK):
+            gather(3, t)
+        group_w(1, 2)
+        group_w(1, 3)
+        quantize_w(1, 0, 4)
+        quantize_x(3)
+        multiply(0)
+        scatter(0)
+        multiply(1)
+        scatter(1)
+        for g in range(PASSES):
+            group_w(2, g)
+        quantize_w(2, 0, 4)
+        multiply(2)
+        group_w(3, 0)
+        group_w(3, 1)
+        quantize_w(3, 0, 2)
+        group_w(3, 2)
+        quantize_w(3, 2, 3)
+        group_w(3, 3)
+        quantize_w(3, 3, 4)
+        scatter(2)
+        multiply(3)
+        scatter(3)
 
         nc.sync.dma_start(out=out, in_=window[:])

@@ -18,6 +18,11 @@ P = 128
 PACK = 4
 K_PASS = P * PACK
 PASSES = K // K_PASS
+COPY = mybir.ActivationFunctionType.Copy
+
+
+S_PASS = 1
+HALF = 256
 
 
 def tile_routed_moe_kernel(tc, xT, w, gate, offs, out):
@@ -42,10 +47,11 @@ def tile_routed_moe_kernel(tc, xT, w, gate, offs, out):
             x_raw.append(raw)
             grouped = held.tile([P, SLOTS, PACK], BF16, name="x_grouped%d" % g, align_bytes=64)
             x_grouped.append(grouped)
+        x_bf = held.tile([P, PACK, T], BF16, name="x_bf")
         w_raw = []
         w_grouped = []
         for e in range(E):
-            raw = held.tile([P, PASSES, PACK * N], F32, name="w_raw%d" % e)
+            raw = held.tile([P, PASSES, PACK * N], F32, name="w_raw%d" % e, tag="w_raw%d" % e)
             w_raw.append(raw)
             grouped = held.tile([P, PASSES, N, PACK], BF16, name="w_grouped%d" % e, align_bytes=64)
             w_grouped.append(grouped)
@@ -54,23 +60,33 @@ def tile_routed_moe_kernel(tc, xT, w, gate, offs, out):
         x_scales = held.tile([P, PASSES, SLOTS], U8, name="x_scales", align_bytes=64)
         w_codes = held.tile([P, E, PASSES * N], U32, name="w_codes", align_bytes=64)
         w_scales = held.tile([P, E, PASSES * N], U8, name="w_scales", align_bytes=64)
-        sums = held.tile([N, SLOTS], F32, name="sums")
 
-        def load_x(g):
-            for t in range(PACK):
-                nc.sync.dma_start(out=x_raw[g][:, t, :], in_=x_view[g, :, t, :])
+        def load_x(g, t):
+            nc.sync.dma_start(out=x_raw[g][:, t, :], in_=x_view[g, :, t, :])
 
         def load_w(e, g0, g1):
             nc.sync.dma_start(out=w_raw[e][:, g0:g1, :], in_=w_view[e, :, g0:g1, :])
 
-        load_x(0)
+        load_x(0, 0)
+        load_x(0, 1)
+        load_x(1, 0)
+        load_x(0, 2)
+        load_x(0, 3)
+        load_x(1, 1)
+        load_x(2, 0)
+        load_x(2, 1)
+        load_x(1, 2)
+        load_x(2, 2)
+        load_x(2, 3)
+        load_x(1, 3)
+        load_x(3, 0)
         load_w(0, 0, 2)
-        load_x(1)
+        load_x(3, 1)
         load_w(0, 2, 4)
-        load_x(2)
+        load_x(3, 2)
         load_w(1, 0, 2)
-        load_x(3)
         load_w(1, 2, 4)
+        load_x(3, 3)
         nc.sync.dma_start(out=gate_sb[:], in_=gate)
         load_w(2, 0, 2)
         load_w(2, 2, 4)
@@ -81,6 +97,15 @@ def tile_routed_moe_kernel(tc, xT, w, gate, offs, out):
         def gather(g, t):
             nc.vector.tensor_copy(x_grouped[g][:, :, t], x_raw[g][:, t, :].indirect(offsets[:]))
 
+        def scalar_gather(g, t):
+            nc.scalar.copy(out=x_bf[:, t, :], in_=x_raw[g][:, t, :])
+            for h in range(SLOTS // HALF):
+                nc.scalar.activation(
+                    x_grouped[g][:, h * HALF : (h + 1) * HALF, t],
+                    x_bf[:, t, :].indirect(offsets[:, h * (HALF // 16) : (h + 1) * (HALF // 16)]),
+                    COPY,
+                )
+
         def quantize_x(g):
             nc.vector.quantize_mx(
                 out=x_codes[:, g, :].bitcast(FP8X4),
@@ -88,11 +113,12 @@ def tile_routed_moe_kernel(tc, xT, w, gate, offs, out):
                 in_=x_grouped[g][:].rearrange("p n t -> p (n t)"),
             )
 
-        def group_w(e, g):
-            nc.scalar.copy(
-                out=w_grouped[e][:, g, :, :].rearrange("p (c i) t -> p c t i", i=4),
-                in_=w_raw[e][:, g, :].rearrange("p (t c i) -> p c t i", t=PACK, i=4),
-            )
+        def group_w(e, g0, g1):
+            for g in range(g0, g1):
+                nc.scalar.copy(
+                    out=w_grouped[e][:, g, :, :].rearrange("p (c i) t -> p c t i", i=4),
+                    in_=w_raw[e][:, g, :].rearrange("p (t c i) -> p c t i", t=PACK, i=4),
+                )
 
         def quantize_w(e, g0, g1):
             nc.vector.quantize_mx(
@@ -101,7 +127,7 @@ def tile_routed_moe_kernel(tc, xT, w, gate, offs, out):
                 in_=w_grouped[e][:, g0:g1, :, :].rearrange("p g n t -> p (g n t)"),
             )
 
-        def multiply(e):
+        def multiply(sums, e):
             acc = psum.tile([N, C], F32, name="acc%d" % e)
             cols = slice(e * C, (e + 1) * C)
             for g in range(PASSES):
@@ -116,7 +142,7 @@ def tile_routed_moe_kernel(tc, xT, w, gate, offs, out):
                 )
             nc.scalar.copy(out=sums[:, cols], in_=acc[:])
 
-        def scatter(e):
+        def scatter(sums, e):
             cols = slice(e * C, (e + 1) * C)
             nc.vector.tensor_tensor(
                 window[:].indirect(offsets[:, e * (C // 16) : (e + 1) * (C // 16)]),
@@ -125,48 +151,41 @@ def tile_routed_moe_kernel(tc, xT, w, gate, offs, out):
                 MULT,
             )
 
-        for t in range(PACK):
-            gather(0, t)
-        group_w(0, 0)
-        group_w(0, 1)
-        gather(1, 0)
-        quantize_x(0)
-        for t in range(1, PACK):
-            gather(1, t)
-        group_w(0, 2)
-        group_w(0, 3)
+        gather(0, 0)
+        gather(0, 1)
+        scalar_gather(1, 0)
+        gather(0, 2)
+        gather(0, 3)
+        scalar_gather(1, 1)
         gather(2, 0)
-        quantize_x(1)
-        quantize_w(0, 0, 4)
-        for t in range(1, PACK):
-            gather(2, t)
-        group_w(1, 0)
-        group_w(1, 1)
+        quantize_x(0)
+        gather(2, 1)
+        scalar_gather(1, 2)
+        gather(2, 2)
+        gather(2, 3)
+        scalar_gather(1, 3)
         gather(3, 0)
         quantize_x(2)
-        for t in range(1, PACK):
-            gather(3, t)
-        group_w(1, 2)
-        group_w(1, 3)
+        quantize_x(1)
+        group_w(0, 0, 4)
+        gather(3, 1)
+        gather(3, 2)
+        quantize_w(0, 0, 4)
+        group_w(1, 0, 4)
+        gather(3, 3)
         quantize_w(1, 0, 4)
         quantize_x(3)
-        multiply(0)
-        scatter(0)
-        multiply(1)
-        scatter(1)
-        for g in range(PASSES):
-            group_w(2, g)
+        group_w(2, 0, 4)
         quantize_w(2, 0, 4)
-        multiply(2)
-        group_w(3, 0)
-        group_w(3, 1)
+        group_w(3, 0, 2)
         quantize_w(3, 0, 2)
-        group_w(3, 2)
+        group_w(3, 2, 3)
         quantize_w(3, 2, 3)
-        group_w(3, 3)
+        group_w(3, 3, 4)
         quantize_w(3, 3, 4)
-        scatter(2)
-        multiply(3)
-        scatter(3)
+        sums = held.tile([N, SLOTS], F32, name="sums", tag="w_raw3")
+        for e in range(E):
+            multiply(sums, e)
+            scatter(sums, e)
 
         nc.sync.dma_start(out=out, in_=window[:])

@@ -21,7 +21,7 @@ PASSES = K // K_PASS
 COPY = mybir.ActivationFunctionType.Copy
 
 
-S_PASS = 1
+S_PLANES = 6
 HALF = 256
 
 
@@ -47,7 +47,7 @@ def tile_routed_moe_kernel(tc, xT, w, gate, offs, out):
             x_raw.append(raw)
             grouped = held.tile([P, SLOTS, PACK], BF16, name="x_grouped%d" % g, align_bytes=64)
             x_grouped.append(grouped)
-        x_bf = held.tile([P, PACK, T], BF16, name="x_bf")
+        x_bf = held.tile([P, S_PLANES, T], BF16, name="x_bf")
         w_raw = []
         w_grouped = []
         for e in range(E):
@@ -68,25 +68,23 @@ def tile_routed_moe_kernel(tc, xT, w, gate, offs, out):
             nc.sync.dma_start(out=w_raw[e][:, g0:g1, :], in_=w_view[e, :, g0:g1, :])
 
         load_x(0, 0)
-        load_x(0, 1)
-        load_x(1, 0)
-        load_x(0, 2)
-        load_x(0, 3)
-        load_x(1, 1)
         load_x(2, 0)
+        load_x(0, 1)
+        load_x(0, 2)
         load_x(2, 1)
-        load_x(1, 2)
+        load_x(0, 3)
+        load_x(1, 0)
         load_x(2, 2)
-        load_x(2, 3)
-        load_x(1, 3)
+        load_x(1, 1)
         load_x(3, 0)
-        load_w(0, 0, 2)
+        load_x(2, 3)
         load_x(3, 1)
-        load_w(0, 2, 4)
+        load_x(1, 2)
         load_x(3, 2)
-        load_w(1, 0, 2)
-        load_w(1, 2, 4)
+        load_x(1, 3)
         load_x(3, 3)
+        load_w(0, 0, 4)
+        load_w(1, 0, 4)
         nc.sync.dma_start(out=gate_sb[:], in_=gate)
         load_w(2, 0, 2)
         load_w(2, 2, 4)
@@ -97,12 +95,12 @@ def tile_routed_moe_kernel(tc, xT, w, gate, offs, out):
         def gather(g, t):
             nc.vector.tensor_copy(x_grouped[g][:, :, t], x_raw[g][:, t, :].indirect(offsets[:]))
 
-        def scalar_gather(g, t):
-            nc.scalar.copy(out=x_bf[:, t, :], in_=x_raw[g][:, t, :])
+        def scalar_gather(g, t, j):
+            nc.gpsimd.tensor_copy(out=x_bf[:, j, :], in_=x_raw[g][:, t, :])
             for h in range(SLOTS // HALF):
                 nc.scalar.activation(
                     x_grouped[g][:, h * HALF : (h + 1) * HALF, t],
-                    x_bf[:, t, :].indirect(offsets[:, h * (HALF // 16) : (h + 1) * (HALF // 16)]),
+                    x_bf[:, j, :].indirect(offsets[:, h * (HALF // 16) : (h + 1) * (HALF // 16)]),
                     COPY,
                 )
 
@@ -113,9 +111,9 @@ def tile_routed_moe_kernel(tc, xT, w, gate, offs, out):
                 in_=x_grouped[g][:].rearrange("p n t -> p (n t)"),
             )
 
-        def group_w(e, g0, g1):
+        def group_w(e, g0, g1, copy=nc.scalar.copy):
             for g in range(g0, g1):
-                nc.scalar.copy(
+                copy(
                     out=w_grouped[e][:, g, :, :].rearrange("p (c i) t -> p c t i", i=4),
                     in_=w_raw[e][:, g, :].rearrange("p (t c i) -> p c t i", t=PACK, i=4),
                 )
@@ -152,40 +150,45 @@ def tile_routed_moe_kernel(tc, xT, w, gate, offs, out):
             )
 
         gather(0, 0)
+        scalar_gather(2, 0, 0)
         gather(0, 1)
-        scalar_gather(1, 0)
         gather(0, 2)
+        scalar_gather(2, 1, 1)
         gather(0, 3)
-        scalar_gather(1, 1)
-        gather(2, 0)
+        gather(1, 0)
         quantize_x(0)
-        gather(2, 1)
-        scalar_gather(1, 2)
-        gather(2, 2)
-        gather(2, 3)
-        scalar_gather(1, 3)
+        scalar_gather(2, 2, 2)
+        gather(1, 1)
         gather(3, 0)
-        quantize_x(2)
-        quantize_x(1)
-        group_w(0, 0, 4)
+        scalar_gather(2, 3, 3)
         gather(3, 1)
+        scalar_gather(1, 2, 4)
         gather(3, 2)
+        quantize_x(2)
+        scalar_gather(1, 3, 5)
+        gather(3, 3)
+        quantize_x(1)
+        quantize_x(3)
+        group_w(0, 0, 4)
         quantize_w(0, 0, 4)
         group_w(1, 0, 4)
-        gather(3, 3)
         quantize_w(1, 0, 4)
-        quantize_x(3)
+        sums = held.tile([N, SLOTS], F32, name="sums", tag="w_raw1")
+        multiply(sums, 0)
+        scatter(sums, 0)
+        multiply(sums, 1)
+        scatter(sums, 1)
         group_w(2, 0, 4)
         quantize_w(2, 0, 4)
-        group_w(3, 0, 2)
-        quantize_w(3, 0, 2)
+        multiply(sums, 2)
+        group_w(3, 0, 2, nc.vector.tensor_copy)
         group_w(3, 2, 3)
+        quantize_w(3, 0, 2)
         quantize_w(3, 2, 3)
         group_w(3, 3, 4)
         quantize_w(3, 3, 4)
-        sums = held.tile([N, SLOTS], F32, name="sums", tag="w_raw3")
-        for e in range(E):
-            multiply(sums, e)
-            scatter(sums, e)
+        scatter(sums, 2)
+        multiply(sums, 3)
+        scatter(sums, 3)
 
         nc.sync.dma_start(out=out, in_=window[:])

@@ -76,15 +76,17 @@ def tile_routed_moe_kernel(tc, xT, w, gate, offs, out):
         load_x(1, 0)
         load_x(2, 2)
         load_x(1, 1)
-        load_x(3, 0)
         load_x(2, 3)
-        load_x(3, 1)
+        load_x(3, 0)
         load_x(1, 2)
-        load_x(3, 2)
+        load_x(3, 1)
         load_x(1, 3)
+        load_x(3, 2)
         load_x(3, 3)
-        load_w(0, 0, 4)
-        load_w(1, 0, 4)
+        load_w(0, 0, 2)
+        load_w(0, 2, 4)
+        load_w(1, 0, 2)
+        load_w(1, 2, 4)
         nc.sync.dma_start(out=gate_sb[:], in_=gate)
         load_w(2, 0, 2)
         load_w(2, 2, 4)
@@ -159,31 +161,34 @@ def tile_routed_moe_kernel(tc, xT, w, gate, offs, out):
         quantize_x(0)
         scalar_gather(2, 2, 2)
         gather(1, 1)
-        gather(3, 0)
         scalar_gather(2, 3, 3)
-        gather(3, 1)
+        gather(3, 0)
         scalar_gather(1, 2, 4)
-        gather(3, 2)
         quantize_x(2)
+        gather(3, 1)
         scalar_gather(1, 3, 5)
+        gather(3, 2)
         gather(3, 3)
         quantize_x(1)
+        group_w(0, 0, 2)
         quantize_x(3)
-        group_w(0, 0, 4)
+        group_w(0, 2, 4)
         quantize_w(0, 0, 4)
-        group_w(1, 0, 4)
+        group_w(1, 0, 2)
+        group_w(1, 2, 4)
         quantize_w(1, 0, 4)
         sums = held.tile([N, SLOTS], F32, name="sums", tag="w_raw1")
         multiply(sums, 0)
         scatter(sums, 0)
         multiply(sums, 1)
         scatter(sums, 1)
-        group_w(2, 0, 4)
+        group_w(2, 0, 2)
+        group_w(2, 2, 4)
         quantize_w(2, 0, 4)
         multiply(sums, 2)
-        group_w(3, 0, 2, nc.vector.tensor_copy)
-        group_w(3, 2, 3)
+        group_w(3, 0, 2)
         quantize_w(3, 0, 2)
+        group_w(3, 2, 3)
         quantize_w(3, 2, 3)
         group_w(3, 3, 4)
         quantize_w(3, 3, 4)

@@ -22,7 +22,6 @@ COPY = mybir.ActivationFunctionType.Copy
 
 
 S_PLANES = 6
-HALF = 256
 
 
 def tile_routed_moe_kernel(tc, xT, w, gate, offs, out):
@@ -99,12 +98,7 @@ def tile_routed_moe_kernel(tc, xT, w, gate, offs, out):
 
         def scalar_gather(g, t, j):
             nc.gpsimd.tensor_copy(out=x_bf[:, j, :], in_=x_raw[g][:, t, :])
-            for h in range(SLOTS // HALF):
-                nc.scalar.activation(
-                    x_grouped[g][:, h * HALF : (h + 1) * HALF, t],
-                    x_bf[:, j, :].indirect(offsets[:, h * (HALF // 16) : (h + 1) * (HALF // 16)]),
-                    COPY,
-                )
+            nc.scalar.activation(x_grouped[g][:, :, t], x_bf[:, j, :].indirect(offsets[:]), COPY)
 
         def quantize_x(g):
             nc.vector.quantize_mx(
@@ -175,18 +169,21 @@ def tile_routed_moe_kernel(tc, xT, w, gate, offs, out):
         group_w(0, 2, 4)
         quantize_w(0, 0, 4)
         group_w(1, 0, 2)
-        group_w(1, 2, 4)
+        group_w(1, 2, 3)
+        group_w(1, 3, 4, nc.vector.tensor_copy)
         quantize_w(1, 0, 4)
         sums = held.tile([N, SLOTS], F32, name="sums", tag="w_raw1")
         multiply(sums, 0)
         scatter(sums, 0)
         multiply(sums, 1)
         scatter(sums, 1)
-        group_w(2, 0, 2)
+        group_w(2, 0, 1)
+        group_w(2, 1, 2, nc.vector.tensor_copy)
         group_w(2, 2, 4)
         quantize_w(2, 0, 4)
         multiply(sums, 2)
-        group_w(3, 0, 2)
+        group_w(3, 0, 1)
+        group_w(3, 1, 2, nc.vector.tensor_copy)
         quantize_w(3, 0, 2)
         group_w(3, 2, 3)
         quantize_w(3, 2, 3)

@@ -31,7 +31,6 @@ def tile_routed_moe_kernel(tc, xT, w, gate, offs, out):
         psum = ctx.enter_context(tc.psum_pool(name="psum", bufs=1))
 
         offsets = held.tile([P, SLOTS // 16], U16, name="offsets")
-        nc.sync.dma_start(offsets[:], offs)
 
         window = held.tile([N, T], F32, name="window")
         nc.vector.memset(window[:], 0.0)
@@ -67,6 +66,7 @@ def tile_routed_moe_kernel(tc, xT, w, gate, offs, out):
             nc.sync.dma_start(out=w_raw[e][:, g0:g1, :], in_=w_view[e, :, g0:g1, :])
 
         load_x(0, 0)
+        nc.sync.dma_start(offsets[:], offs)
         load_x(2, 0)
         load_x(0, 1)
         load_x(0, 2)
@@ -86,12 +86,13 @@ def tile_routed_moe_kernel(tc, xT, w, gate, offs, out):
         load_w(0, 2, 4)
         load_w(1, 0, 2)
         load_w(1, 2, 4)
-        nc.sync.dma_start(out=gate_sb[:], in_=gate)
+        nc.sync.dma_start(out=gate_sb[:, : SLOTS // 2], in_=gate[:, : SLOTS // 2])
         load_w(2, 0, 2)
         load_w(2, 2, 4)
         load_w(3, 0, 2)
         load_w(3, 2, 3)
         load_w(3, 3, 4)
+        nc.sync.dma_start(out=gate_sb[:, SLOTS // 2 :], in_=gate[:, SLOTS // 2 :])
 
         def gather(g, t):
             nc.vector.tensor_copy(x_grouped[g][:, :, t], x_raw[g][:, t, :].indirect(offsets[:]))

@@ -67,8 +67,8 @@ def tile_routed_moe_kernel(tc, xT, w, gate, offs, out):
 
         load_x(0, 0)
         nc.sync.dma_start(offsets[:], offs)
-        load_x(2, 0)
         load_x(0, 1)
+        load_x(2, 0)
         load_x(0, 2)
         load_x(2, 1)
         load_x(0, 3)
@@ -76,12 +76,12 @@ def tile_routed_moe_kernel(tc, xT, w, gate, offs, out):
         load_x(2, 2)
         load_x(1, 1)
         load_x(2, 3)
-        load_x(3, 0)
         load_x(1, 2)
-        load_x(3, 1)
-        load_x(1, 3)
         load_x(3, 2)
+        load_x(1, 3)
         load_x(3, 3)
+        load_x(3, 0)
+        load_x(3, 1)
         load_w(0, 0, 2)
         load_w(0, 2, 4)
         load_w(1, 0, 2)
@@ -147,8 +147,8 @@ def tile_routed_moe_kernel(tc, xT, w, gate, offs, out):
             )
 
         gather(0, 0)
-        scalar_gather(2, 0, 0)
         gather(0, 1)
+        scalar_gather(2, 0, 0)
         gather(0, 2)
         scalar_gather(2, 1, 1)
         gather(0, 3)
@@ -157,14 +157,14 @@ def tile_routed_moe_kernel(tc, xT, w, gate, offs, out):
         scalar_gather(2, 2, 2)
         gather(1, 1)
         scalar_gather(2, 3, 3)
-        gather(3, 0)
-        scalar_gather(1, 2, 4)
+        gather(1, 2)
+        scalar_gather(3, 2, 4)
         quantize_x(2)
-        gather(3, 1)
-        scalar_gather(1, 3, 5)
-        gather(3, 2)
-        gather(3, 3)
+        gather(1, 3)
+        scalar_gather(3, 3, 5)
+        gather(3, 0)
         quantize_x(1)
+        gather(3, 1)
         group_w(0, 0, 2)
         quantize_x(3)
         group_w(0, 2, 4)

@@ -115,6 +115,12 @@ def tile_routed_moe_kernel(tc, xT, w, gate, offs, out):
                     in_=w_raw[e][:, g, :].rearrange("p (t c i) -> p c t i", t=PACK, i=4),
                 )
 
+        def group_w_pool(e, g):
+            nc.gpsimd.tensor_copy(
+                out=w_grouped[e][:, g, :, :],
+                in_=w_raw[e][:, g, :].rearrange("p (t n) -> p n t", t=PACK),
+            )
+
         def quantize_w(e, g0, g1):
             nc.vector.quantize_mx(
                 out=w_codes[:, e, g0 * N : g1 * N].bitcast(FP8X4),
@@ -122,8 +128,10 @@ def tile_routed_moe_kernel(tc, xT, w, gate, offs, out):
                 in_=w_grouped[e][:, g0:g1, :, :].rearrange("p g n t -> p (g n t)"),
             )
 
-        def multiply(sums, e):
-            acc = psum.tile([N, C], F32, name="acc%d" % e)
+        accs = [psum.tile([N, C], F32, name="acc%d" % e) for e in range(E)]
+
+        def matmuls(e):
+            acc = accs[e]
             cols = slice(e * C, (e + 1) * C)
             for g in range(PASSES):
                 nc.tensor.matmul_mx(
@@ -135,14 +143,15 @@ def tile_routed_moe_kernel(tc, xT, w, gate, offs, out):
                     start=(g == 0),
                     stop=(g == PASSES - 1),
                 )
-            nc.scalar.copy(out=sums[:, cols], in_=acc[:])
 
-        def scatter(sums, e):
-            cols = slice(e * C, (e + 1) * C)
+        def finish(e):
+            tag = "w_raw%d" % (e + 1) if e + 1 < E else "sums_last"
+            sums = held.tile([N, C], F32, name="sums%d" % e, tag=tag)
+            nc.scalar.copy(out=sums[:], in_=accs[e][:])
             nc.vector.tensor_tensor(
                 window[:].indirect(offsets[:, e * (C // 16) : (e + 1) * (C // 16)]),
-                sums[:, cols],
-                gate_sb[:, cols],
+                sums[:],
+                gate_sb[:, e * C : (e + 1) * C],
                 MULT,
             )
 
@@ -169,29 +178,26 @@ def tile_routed_moe_kernel(tc, xT, w, gate, offs, out):
         quantize_x(3)
         group_w(0, 2, 4)
         quantize_w(0, 0, 4)
-        group_w(1, 0, 2)
-        group_w(1, 2, 3)
+        matmuls(0)
+        group_w(1, 0, 3)
         group_w(1, 3, 4, nc.vector.tensor_copy)
+        finish(0)
         quantize_w(1, 0, 4)
-        sums = held.tile([N, SLOTS], F32, name="sums", tag="w_raw1")
-        multiply(sums, 0)
-        scatter(sums, 0)
-        multiply(sums, 1)
-        scatter(sums, 1)
-        group_w(2, 0, 1)
-        group_w(2, 1, 2, nc.vector.tensor_copy)
-        group_w(2, 2, 4)
+        matmuls(1)
+        group_w(2, 0, 3)
+        group_w(2, 3, 4, nc.vector.tensor_copy)
+        finish(1)
         quantize_w(2, 0, 4)
-        multiply(sums, 2)
+        matmuls(2)
         group_w(3, 0, 1)
-        group_w(3, 1, 2, nc.vector.tensor_copy)
+        group_w_pool(3, 1)
         quantize_w(3, 0, 2)
         group_w(3, 2, 3)
         quantize_w(3, 2, 3)
         group_w(3, 3, 4)
+        finish(2)
         quantize_w(3, 3, 4)
-        scatter(sums, 2)
-        multiply(sums, 3)
-        scatter(sums, 3)
+        matmuls(3)
+        finish(3)
 
         nc.sync.dma_start(out=out, in_=window[:])

@@ -21,7 +21,7 @@ PASSES = K // K_PASS
 COPY = mybir.ActivationFunctionType.Copy
 
 
-S_PLANES = 6
+S_PLANES = 8
 
 
 def tile_routed_moe_kernel(tc, xT, w, gate, offs, out):
@@ -65,23 +65,16 @@ def tile_routed_moe_kernel(tc, xT, w, gate, offs, out):
         def load_w(e, g0, g1):
             nc.sync.dma_start(out=w_raw[e][:, g0:g1, :], in_=w_view[e, :, g0:g1, :])
 
-        load_x(0, 0)
-        nc.sync.dma_start(offsets[:], offs)
-        load_x(0, 1)
-        load_x(2, 0)
-        load_x(0, 2)
-        load_x(2, 1)
-        load_x(0, 3)
-        load_x(1, 0)
-        load_x(2, 2)
-        load_x(1, 1)
-        load_x(2, 3)
-        load_x(1, 2)
-        load_x(3, 2)
-        load_x(1, 3)
-        load_x(3, 3)
-        load_x(3, 0)
-        load_x(3, 1)
+        plane_order = [
+            (0, 0), (0, 2), (0, 3), (0, 1),
+            (1, 2), (1, 0), (1, 3), (1, 1),
+            (2, 2), (2, 3), (2, 0), (3, 2),
+            (2, 1), (3, 3), (3, 0), (3, 1),
+        ]
+        for i, (g, t) in enumerate(plane_order):
+            load_x(g, t)
+            if i == 0:
+                nc.sync.dma_start(offsets[:], offs)
         load_w(0, 0, 2)
         load_w(0, 2, 4)
         load_w(1, 0, 2)
@@ -155,25 +148,17 @@ def tile_routed_moe_kernel(tc, xT, w, gate, offs, out):
                 MULT,
             )
 
-        gather(0, 0)
-        gather(0, 1)
-        scalar_gather(2, 0, 0)
-        gather(0, 2)
-        scalar_gather(2, 1, 1)
-        gather(0, 3)
-        gather(1, 0)
-        quantize_x(0)
-        scalar_gather(2, 2, 2)
-        gather(1, 1)
-        scalar_gather(2, 3, 3)
-        gather(1, 2)
-        scalar_gather(3, 2, 4)
-        quantize_x(2)
-        gather(1, 3)
-        scalar_gather(3, 3, 5)
-        gather(3, 0)
-        quantize_x(1)
-        gather(3, 1)
+        landed = [0] * PASSES
+        casts = 0
+        for g, t in plane_order:
+            if t < 2:
+                gather(g, t)
+            else:
+                scalar_gather(g, t, casts)
+                casts += 1
+            landed[g] += 1
+            if landed[g] == PACK and g < PASSES - 1:
+                quantize_x(g)
         group_w(0, 0, 2)
         quantize_x(3)
         group_w(0, 2, 4)

@@ -59,20 +59,20 @@ def tile_routed_moe_kernel(tc, xT, w, gate, offs, out):
         w_codes = held.tile([P, E, PASSES * N], U32, name="w_codes", align_bytes=64)
         w_scales = held.tile([P, E, PASSES * N], U8, name="w_scales", align_bytes=64)
 
-        def load_x(g, t):
-            nc.sync.dma_start(out=x_raw[g][:, t, :], in_=x_view[g, :, t, :])
+        def load_x(g, t0, t1):
+            nc.sync.dma_start(out=x_raw[g][:, t0:t1, :], in_=x_view[g, :, t0:t1, :])
 
         def load_w(e, g0, g1):
             nc.sync.dma_start(out=w_raw[e][:, g0:g1, :], in_=w_view[e, :, g0:g1, :])
 
-        plane_order = [
-            (0, 0), (0, 2), (0, 3), (0, 1),
-            (1, 2), (1, 0), (1, 3), (1, 1),
-            (2, 2), (2, 3), (2, 0), (3, 2),
-            (2, 1), (3, 3), (3, 0), (3, 1),
+        x_loads = [
+            (0, 2, 4), (0, 0, 1), (0, 1, 2),
+            (1, 2, 4), (1, 0, 2),
+            (2, 2, 4), (2, 0, 2),
+            (3, 2, 3), (3, 3, 4), (3, 0, 1), (3, 1, 2),
         ]
-        for i, (g, t) in enumerate(plane_order):
-            load_x(g, t)
+        for i, (g, t0, t1) in enumerate(x_loads):
+            load_x(g, t0, t1)
             if i == 0:
                 nc.sync.dma_start(offsets[:], offs)
         load_w(0, 0, 2)
@@ -150,7 +150,7 @@ def tile_routed_moe_kernel(tc, xT, w, gate, offs, out):
 
         landed = [0] * PASSES
         casts = 0
-        for g, t in plane_order:
+        for g, t in [(g, t) for g, t0, t1 in x_loads for t in range(t0, t1)]:
             if t < 2:
                 gather(g, t)
             else:

@@ -169,10 +169,12 @@ def tile_routed_moe_kernel(tc, xT, w, gate, offs, out):
         finish(0)
         quantize_w(1, 0, 4)
         matmuls(1)
-        group_w(2, 0, 3)
+        group_w(2, 0, 2)
+        quantize_w(2, 0, 2)
+        group_w(2, 2, 3)
         group_w(2, 3, 4, nc.vector.tensor_copy)
         finish(1)
-        quantize_w(2, 0, 4)
+        quantize_w(2, 2, 4)
         matmuls(2)
         group_w(3, 0, 1)
         group_w_pool(3, 1)

from contextlib import ExitStack

import concourse.mybir as mybir

K, T, E, C, N = 2048, 1024, 4, 128, 128
SLOTS = E * C
FLOPS = 2 * K * N * SLOTS

F32 = mybir.dt.float32
BF16 = mybir.dt.bfloat16
U32 = mybir.dt.uint32
U16 = mybir.dt.uint16
U8 = mybir.dt.uint8
FP8X4 = mybir.dt.float8_e4m3fn_x4
MULT = mybir.AluOpType.mult

P = 128
PACK = 4
K_PASS = P * PACK
PASSES = K // K_PASS
COPY = mybir.ActivationFunctionType.Copy


S_PLANES = 8


def tile_routed_moe_kernel(tc, xT, w, gate, offs, out):
    nc = tc.nc
    with ExitStack() as ctx:
        held = ctx.enter_context(tc.tile_pool(name="held", bufs=1))
        psum = ctx.enter_context(tc.psum_pool(name="psum", bufs=1))

        offsets = held.tile([P, SLOTS // 16], U16, name="offsets")

        window = held.tile([N, T], F32, name="window")
        nc.vector.memset(window[:], 0.0)

        x_view = xT.rearrange("(g p t) n -> g p t n", p=P, t=PACK)
        w_view = w.rearrange("e (g p t) n -> e p g (t n)", p=P, t=PACK)

        x_raw = []
        x_grouped = []
        for g in range(PASSES):
            raw = held.tile([P, PACK, T], F32, name="x_raw%d" % g)
            x_raw.append(raw)
            grouped = held.tile([P, SLOTS, PACK], BF16, name="x_grouped%d" % g, align_bytes=64)
            x_grouped.append(grouped)
        x_bf = held.tile([P, S_PLANES, T], BF16, name="x_bf")
        w_raw = []
        w_grouped = []
        for e in range(E):
            raw = held.tile([P, PASSES, PACK * N], F32, name="w_raw%d" % e, tag="w_raw%d" % e)
            w_raw.append(raw)
            grouped = held.tile([P, PASSES, N, PACK], BF16, name="w_grouped%d" % e, align_bytes=64)
            w_grouped.append(grouped)
        gate_sb = held.tile([N, SLOTS], F32, name="gate_sb")
        x_codes = held.tile([P, PASSES, SLOTS], U32, name="x_codes", align_bytes=64)
        x_scales = held.tile([P, PASSES, SLOTS], U8, name="x_scales", align_bytes=64)
        w_codes = held.tile([P, E, PASSES * N], U32, name="w_codes", align_bytes=64)
        w_scales = held.tile([P, E, PASSES * N], U8, name="w_scales", align_bytes=64)

        def load_x(g, t0, t1):
            nc.sync.dma_start(out=x_raw[g][:, t0:t1, :], in_=x_view[g, :, t0:t1, :])

        def load_w(e, g0, g1):
            nc.sync.dma_start(out=w_raw[e][:, g0:g1, :], in_=w_view[e, :, g0:g1, :])

        x_loads = [
            (0, 2, 4), (0, 0, 1), (0, 1, 2),
            (1, 2, 4), (1, 0, 2),
            (2, 2, 4), (2, 0, 2),
            (3, 2, 3), (3, 3, 4), (3, 0, 1), (3, 1, 2),
        ]
        for i, (g, t0, t1) in enumerate(x_loads):
            load_x(g, t0, t1)
            if i == 0:
                nc.sync.dma_start(offsets[:], offs)
        load_w(0, 0, 2)
        load_w(0, 2, 4)
        load_w(1, 0, 2)
        load_w(1, 2, 4)
        nc.sync.dma_start(out=gate_sb[:, : SLOTS // 2], in_=gate[:, : SLOTS // 2])
        load_w(2, 0, 2)
        load_w(2, 2, 4)
        load_w(3, 0, 2)
        load_w(3, 2, 3)
        load_w(3, 3, 4)
        nc.sync.dma_start(out=gate_sb[:, SLOTS // 2 :], in_=gate[:, SLOTS // 2 :])

        def gather(g, t):
            nc.vector.tensor_copy(x_grouped[g][:, :, t], x_raw[g][:, t, :].indirect(offsets[:]))

        def scalar_gather(g, t, j):
            nc.gpsimd.tensor_copy(out=x_bf[:, j, :], in_=x_raw[g][:, t, :])
            nc.scalar.activation(x_grouped[g][:, :, t], x_bf[:, j, :].indirect(offsets[:]), COPY)

        def quantize_x(g):
            nc.vector.quantize_mx(
                out=x_codes[:, g, :].bitcast(FP8X4),
                scales=x_scales[:, g, :],
                in_=x_grouped[g][:].rearrange("p n t -> p (n t)"),
            )

        def group_w(e, g0, g1, copy=nc.scalar.copy):
            for g in range(g0, g1):
                copy(
                    out=w_grouped[e][:, g, :, :].rearrange("p (c i) t -> p c t i", i=4),
                    in_=w_raw[e][:, g, :].rearrange("p (t c i) -> p c t i", t=PACK, i=4),
                )

        def group_w_pool(e, g):
            nc.gpsimd.tensor_copy(
                out=w_grouped[e][:, g, :, :],
                in_=w_raw[e][:, g, :].rearrange("p (t n) -> p n t", t=PACK),
            )

        def quantize_w(e, g0, g1):
            nc.vector.quantize_mx(
                out=w_codes[:, e, g0 * N : g1 * N].bitcast(FP8X4),
                scales=w_scales[:, e, g0 * N : g1 * N],
                in_=w_grouped[e][:, g0:g1, :, :].rearrange("p g n t -> p (g n t)"),
            )

        accs = [psum.tile([N, C], F32, name="acc%d" % e) for e in range(E)]

        def matmuls(e):
            acc = accs[e]
            cols = slice(e * C, (e + 1) * C)
            for g in range(PASSES):
                nc.tensor.matmul_mx(
                    out=acc[:],
                    lhsT=w_codes[:, e, g * N : (g + 1) * N].bitcast(FP8X4),
                    lhsT_scale=w_scales[:, e, g * N : (g + 1) * N],
                    rhs=x_codes[:, g, cols].bitcast(FP8X4),
                    rhs_scale=x_scales[:, g, cols],
                    start=(g == 0),
                    stop=(g == PASSES - 1),
                )

        def finish(e):
            tag = "w_raw%d" % (e + 1) if e + 1 < E else "sums_last"
            sums = held.tile([N, C], F32, name="sums%d" % e, tag=tag)
            nc.scalar.copy(out=sums[:], in_=accs[e][:])
            nc.vector.tensor_tensor(
                window[:].indirect(offsets[:, e * (C // 16) : (e + 1) * (C // 16)]),
                sums[:],
                gate_sb[:, e * C : (e + 1) * C],
                MULT,
            )

        landed = [0] * PASSES
        casts = 0
        for g, t in [(g, t) for g, t0, t1 in x_loads for t in range(t0, t1)]:
            if t < 2:
                gather(g, t)
            else:
                scalar_gather(g, t, casts)
                casts += 1
            landed[g] += 1
            if landed[g] == PACK and g < PASSES - 1:
                quantize_x(g)
        group_w(0, 0, 2)
        quantize_x(3)
        group_w(0, 2, 4)
        quantize_w(0, 0, 4)
        matmuls(0)
        group_w(1, 0, 3)
        group_w(1, 3, 4, nc.vector.tensor_copy)
        finish(0)
        quantize_w(1, 0, 4)
        matmuls(1)
        group_w(2, 0, 2)
        quantize_w(2, 0, 2)
        group_w(2, 2, 3)
        group_w(2, 3, 4, nc.vector.tensor_copy)
        finish(1)
        quantize_w(2, 2, 4)
        matmuls(2)
        group_w(3, 0, 1)
        group_w_pool(3, 1)
        quantize_w(3, 0, 2)
        group_w(3, 2, 3)
        quantize_w(3, 2, 3)
        group_w(3, 3, 4)
        finish(2)
        quantize_w(3, 3, 4)
        matmuls(3)
        finish(3)

        nc.sync.dma_start(out=out, in_=window[:])
